import numpy as np
import ml_dtypes


def mxq(x, axis, fmt="e4m3"):
    dtype, down = {"e4m3": (ml_dtypes.float8_e4m3fn, 7), "e5m2": (ml_dtypes.float8_e5m2, 14)}[fmt]
    v = np.moveaxis(np.asarray(x, np.float32).astype(ml_dtypes.bfloat16).astype(np.float64), axis, -1)
    blocks = v.reshape(v.shape[:-1] + (-1, 32))
    amax = np.abs(blocks).max(-1, keepdims=True)
    byte = np.maximum(np.where(amax > 0, np.frexp(amax)[1] - 1 + 127, 0) - down, 1)
    scale = np.exp2(byte - 127.0)
    codes = (blocks / scale).astype(np.float32).astype(dtype).astype(np.float64)
    return np.moveaxis((codes * scale).reshape(v.shape), -1, axis)


WIDE = False


def mx_kscale(k):
    if not WIDE:
        return np.ones(k)
    levels = np.array([10, -10, 5, -5, 0])
    if k % 512:
        return np.exp2(np.random.permutation(np.resize(levels, k // 32))).repeat(32)
    a = np.empty((k // 512, 16))
    for p in range(k // 512):
        a[p, :8] = np.random.permutation(np.resize(levels, 8))
        for g in range(8):
            far = levels[np.abs(levels - a[p, g]) >= 10]
            a[p, g + 8] = far[np.random.randint(len(far))]
    return np.exp2(a.ravel()).repeat(32)


def f64(x):
    return np.asarray(x).astype(np.float64)


def striped(idx):
    return np.tile(np.asarray(idx).reshape(-1, 16).T, (8, 1)).astype(np.uint16)


def unstriped(offs):
    return offs[:16].T.reshape(-1).astype(np.int64)


E2M1 = np.array([0.0, 0.5, 1.0, 1.5, 2.0, 3.0, 4.0, 6.0, -0.0, -0.5, -1.0, -1.5, -2.0, -3.0, -4.0, -6.0])


def pack_weight(w, fmt):
    k, n = w.shape
    w = f64(np.asarray(w, np.float32).astype(ml_dtypes.bfloat16)).reshape(k // 32, 32, n)
    amax = np.abs(w).max(1)
    if fmt == "e4m3":
        byte = np.frexp(amax)[1] - 1 + 127 - 7
    else:
        mant, ex = np.frexp(amax / 6.0)
        byte = np.where(mant > 0.5, ex, ex - 1) + 127
    byte = np.clip(np.where(amax > 0, byte, 1), 1, 254)
    scaled = (w * np.exp2(127.0 - byte)[:, None, :]).reshape(k, n).astype(np.float32)
    by_word = np.ascontiguousarray(scaled.reshape(k // 512, 128, 4, n).transpose(0, 1, 3, 2))
    if fmt == "e4m3":
        words = by_word.astype(ml_dtypes.float8_e4m3fn).view(np.uint8)
    else:
        c = by_word.astype(ml_dtypes.float4_e2m1fn).view(np.uint8) & 0xF
        words = (c[..., 0::2] | (c[..., 1::2] << 4)).reshape(k // 512, 128, 2 * n)
    return np.ascontiguousarray(words), np.ascontiguousarray(byte.astype(np.uint8).reshape(k // 512, 16, n))


def unpack_weight(words, scales, fmt):
    g, _, n = scales.shape
    words = np.ascontiguousarray(words).reshape(g, 128, n, -1)
    if fmt == "e4m3":
        vals = words.view(ml_dtypes.float8_e4m3fn).astype(np.float64)
    else:
        nib = np.empty((g, 128, n, 4), np.uint8)
        nib[..., 0::2] = words & 0xF
        nib[..., 1::2] = words >> 4
        vals = E2M1[nib]
    vals = vals * np.repeat(np.exp2(scales.astype(np.float64) - 127.0), 8, axis=1)[..., None]
    return vals.transpose(0, 1, 3, 2).reshape(g * 512, n)


B, N, T, D, NQ = 2, 512, 2048, 512, 128


def setup_inputs():
    n = np.random.standard_normal
    pages = np.random.permutation(T // 32)[:B * N // 32]
    idx = (pages[:, None] * 32 + np.arange(32)[None, :]).reshape(-1)
    s = mx_kscale(D)[:, None]
    kp = pack_weight(n((D, T)) / s, "e4m3")
    return {
        "qT": (n((B, D, NQ)) * s * (1.00 / np.sqrt(D))).astype(np.float32),
        "k_words": kp[0],
        "k_scales": kp[1],
        "sk": (n((B, NQ, 1))).astype(np.float32),
        "offs": striped(idx),
    }


def reference(qT, k_words, k_scales, sk, offs):
    idx = unstriped(offs)
    pick = lambda x, which: x[:, which].reshape(x.shape[0], B, -1).transpose(1, 0, 2)
    k = unpack_weight(k_words, k_scales, "e4m3")
    kg = pick(k, idx)
    qq = mxq(f64(qT), 1, "e4m3")
    a = qq.transpose(0, 2, 1) @ kg
    m = np.maximum(np.max(a, axis=-1, keepdims=True), f64(sk))
    e = np.exp(a - m)
    y = e / (np.sum(e, axis=-1, keepdims=True) + np.exp(f64(sk) - m))
    return y

@@ -1,0 +1,139 @@
+from contextlib import ExitStack
+
+import concourse.mybir as mybir
+
+B, N, T, D, NQ = 2, 512, 2048, 512, 128
+FLOPS = 2 * B * NQ * N * D
+
+F32 = mybir.dt.float32
+BF16 = mybir.dt.bfloat16
+I32 = mybir.dt.int32
+U32 = mybir.dt.uint32
+U16 = mybir.dt.uint16
+U8 = mybir.dt.uint8
+FP8X4 = mybir.dt.float8_e4m3fn_x4
+ALU = mybir.AluOpType
+ACT = mybir.ActivationFunctionType
+
+P = 128
+PACK = 4
+HALF = N // 2
+ROW = N + 8
+
+
+def tile_attend_wtsink_kernel(tc, qT, k_words, k_scales, sk, offs, out):
+    nc = tc.nc
+    with ExitStack() as ctx:
+        lists = ctx.enter_context(tc.tile_pool(name="lists", bufs=1))
+        sb = ctx.enter_context(tc.tile_pool(name="sb", bufs=1))
+        psum = ctx.enter_context(tc.psum_pool(name="psum", bufs=1))
+
+        offsets = lists.tile([P, B * N // 16], U16, name="offsets")
+        pool_words = sb.tile([P, T], I32, name="pool_words", align_bytes=64)
+        pool_scales = sb.tile([P, T // 4], I32, name="pool_scales", align_bytes=64)
+        q_raw = [sb.tile([P, PACK, NQ], F32, name=f"q_raw{b}") for b in range(B)]
+        q_bf = [sb.tile([P, NQ, PACK], BF16, name=f"q_bf{b}", align_bytes=64) for b in range(B)]
+        q_codes = [sb.tile([P, NQ], U32, name=f"q_codes{b}", align_bytes=64) for b in range(B)]
+        q_scales = [sb.tile([P, NQ], U8, name=f"q_scales{b}", align_bytes=64) for b in range(B)]
+        key_scales = [sb.tile([P, N], U8, name=f"key_scales{b}", align_bytes=64) for b in range(B)]
+        key_words = [[sb.tile([P, HALF], U32, name=f"key_words{b}_{h}", align_bytes=64) for h in range(2)] for b in range(B)]
+        sinks = sb.tile([P, B], F32, name="sinks")
+        neg = [sb.tile([P, ROW], F32, name=f"neg{b}") for b in range(B)]
+        neg_max = [sb.tile([P, 1], F32, name=f"neg_max{b}") for b in range(B)]
+        e = [sb.tile([P, ROW], F32, name=f"e{b}") for b in range(B)]
+        total = [sb.tile([P, 1], F32, name=f"total{b}") for b in range(B)]
+        inv = [sb.tile([P, 1], F32, name=f"inv{b}") for b in range(B)]
+        y = [sb.tile([P, N], F32, name=f"y{b}") for b in range(B)]
+        warm_in = sb.tile([P, 1], F32, name="warm_in")
+        warm_out = sb.tile([P, 1], F32, name="warm_out")
+        scores = [psum.tile([P, N], F32, name=f"scores{b}") for b in range(B)]
+
+        nc.vector.memset(pool_scales[:], 0)
+        nc.vector.memset(warm_in[:], 0.0)
+
+        nc.sync.dma_start(q_raw[0][:], qT[0].rearrange("(p j) w -> p j w", j=PACK))
+        nc.scalar.dma_start(q_raw[1][:], qT[1].rearrange("(p j) w -> p j w", j=PACK))
+        nc.sync.dma_start(offsets[:], offs)
+        scale_rows = k_scales[0].bitcast(I32)
+        for r in range(4):
+            nc.sync.dma_start(pool_scales[r:P:32, :], scale_rows[r:16:4, :])
+        nc.sync.dma_start(pool_words[:], k_words[0].rearrange("p n t -> p (n t)").bitcast(I32))
+        with nc.allow_non_contiguous_dma(reason="one sink a query row"):
+            nc.sync.dma_start(sinks[:], sk.rearrange("b q o -> q (b o)"))
+
+        nc.scalar.activation(warm_out[:], warm_in[:], ACT.Exp)
+
+        def quantize_queries(b):
+            nc.vector.quantize_mx(
+                out=q_codes[b][:].bitcast(FP8X4),
+                scales=q_scales[b][:],
+                in_=q_bf[b][:].rearrange("p w j -> p (w j)"),
+            )
+
+        def gather_words(b, h):
+            c0 = (b * N + h * HALF) // 16
+            nc.vector.tensor_copy(
+                key_words[b][h][:], pool_words[:].bitcast(U32).indirect(offsets[:, c0 : c0 + HALF // 16])
+            )
+
+        def score(b, h):
+            cols = slice(h * HALF, (h + 1) * HALF)
+            nc.tensor.matmul_mx(
+                out=scores[b][:, cols],
+                lhsT=q_codes[b][:].bitcast(FP8X4),
+                lhsT_scale=q_scales[b][:],
+                rhs=key_words[b][h][:].bitcast(FP8X4),
+                rhs_scale=key_scales[b][:, cols],
+                start=True,
+                stop=True,
+            )
+
+        def gather_scales(b):
+            c0 = b * N // 16
+            nc.vector.tensor_copy(
+                key_scales[b][:], pool_scales[:].bitcast(U8).indirect(offsets[:, c0 : c0 + N // 16])
+            )
+
+        nc.vector.tensor_copy(q_bf[0][:], q_raw[0][:].rearrange("p j w -> p w j"))
+        gather_scales(0)
+        quantize_queries(0)
+        nc.scalar.copy(q_bf[1][:], q_raw[1][:].rearrange("p j w -> p w j"))
+        quantize_queries(1)
+        gather_scales(1)
+        for b in range(B):
+            nc.scalar.activation(neg[b][:, N : N + 1], sinks[:, b : b + 1], ACT.Copy, scale=-1.0)
+
+        for b in range(B):
+            for h in range(2):
+                gather_words(b, h)
+                score(b, h)
+
+        for b in range(B):
+            nc.vector.tensor_scalar(
+                out=neg[b][:, 0:N],
+                in0=scores[b][:],
+                scalar1=-1.0,
+                scalar2=neg[b][:, N : N + 1],
+                op0=ALU.mult,
+                op1=ALU.min,
+                accum_out=neg_max[b][:],
+            )
+            nc.scalar.activation(
+                e[b][:, 0 : N + 1],
+                neg[b][:, 0 : N + 1],
+                ACT.Exp,
+                bias=neg_max[b][:],
+                scale=-1.0,
+                accum_out=total[b][:],
+            )
+        for b in range(B):
+            nc.vector.reciprocal(inv[b][:], total[b][:])
+            pieces = 1 if b == 0 else 2
+            width = N // pieces
+            for h in range(pieces):
+                cols = slice(h * width, (h + 1) * width)
+                nc.vector.tensor_scalar(
+                    out=y[b][:, cols], in0=e[b][:, cols], scalar1=inv[b][:], scalar2=None, op0=ALU.mult
+                )
+                queue = nc.scalar if h == 1 else nc.sync
+                queue.dma_start(out[b][:, cols], y[b][:, cols])

@@ -17,6 +17,9 @@ ACT = mybir.ActivationFunctionType
 
 P = 128
 PACK = 4
+PER_COLUMN = 16
+QUADRANT = 32
+SCALE_ROWS = D // 32
 HALF = N // 2
 ROW = N + 8
 
@@ -28,15 +31,17 @@ def tile_attend_wtsink_kernel(tc, qT, k_words, k_scales, sk, offs, out):
         sb = ctx.enter_context(tc.tile_pool(name="sb", bufs=1))
         psum = ctx.enter_context(tc.psum_pool(name="psum", bufs=1))
 
-        offsets = lists.tile([P, B * N // 16], U16, name="offsets")
+        offsets = lists.tile([P, B * N // PER_COLUMN], U16, name="offsets")
         pool_words = sb.tile([P, T], I32, name="pool_words", align_bytes=64)
-        pool_scales = sb.tile([P, T // 4], I32, name="pool_scales", align_bytes=64)
+        pool_scales = sb.tile([P, T // PACK], I32, name="pool_scales", align_bytes=64)
         q_raw = [sb.tile([P, PACK, NQ], F32, name=f"q_raw{b}") for b in range(B)]
         q_bf = [sb.tile([P, NQ, PACK], BF16, name=f"q_bf{b}", align_bytes=64) for b in range(B)]
         q_codes = [sb.tile([P, NQ], U32, name=f"q_codes{b}", align_bytes=64) for b in range(B)]
         q_scales = [sb.tile([P, NQ], U8, name=f"q_scales{b}", align_bytes=64) for b in range(B)]
         key_scales = [sb.tile([P, N], U8, name=f"key_scales{b}", align_bytes=64) for b in range(B)]
-        key_words = [[sb.tile([P, HALF], U32, name=f"key_words{b}_{h}", align_bytes=64) for h in range(2)] for b in range(B)]
+        key_words = [
+            [sb.tile([P, HALF], U32, name=f"key_words{b}_{h}", align_bytes=64) for h in range(2)] for b in range(B)
+        ]
         sinks = sb.tile([P, B], F32, name="sinks")
         neg = [sb.tile([P, ROW], F32, name=f"neg{b}") for b in range(B)]
         neg_max = [sb.tile([P, 1], F32, name=f"neg_max{b}") for b in range(B)]
@@ -44,24 +49,19 @@ def tile_attend_wtsink_kernel(tc, qT, k_words, k_scales, sk, offs, out):
         total = [sb.tile([P, 1], F32, name=f"total{b}") for b in range(B)]
         inv = [sb.tile([P, 1], F32, name=f"inv{b}") for b in range(B)]
         y = [sb.tile([P, N], F32, name=f"y{b}") for b in range(B)]
-        warm_in = sb.tile([P, 1], F32, name="warm_in")
-        warm_out = sb.tile([P, 1], F32, name="warm_out")
         scores = [psum.tile([P, N], F32, name=f"scores{b}") for b in range(B)]
 
         nc.vector.memset(pool_scales[:], 0)
-        nc.vector.memset(warm_in[:], 0.0)
 
         nc.sync.dma_start(q_raw[0][:], qT[0].rearrange("(p j) w -> p j w", j=PACK))
         nc.scalar.dma_start(q_raw[1][:], qT[1].rearrange("(p j) w -> p j w", j=PACK))
         nc.sync.dma_start(offsets[:], offs)
         scale_rows = k_scales[0].bitcast(I32)
         for r in range(4):
-            nc.sync.dma_start(pool_scales[r:P:32, :], scale_rows[r:16:4, :])
+            nc.sync.dma_start(pool_scales[r:P:QUADRANT, :], scale_rows[r:SCALE_ROWS:4, :])
         nc.sync.dma_start(pool_words[:], k_words[0].rearrange("p n t -> p (n t)").bitcast(I32))
         with nc.allow_non_contiguous_dma(reason="one sink a query row"):
             nc.sync.dma_start(sinks[:], sk.rearrange("b q o -> q (b o)"))
-
-        nc.scalar.activation(warm_out[:], warm_in[:], ACT.Exp)
 
         def quantize_queries(b):
             nc.vector.quantize_mx(
@@ -70,10 +70,16 @@ def tile_attend_wtsink_kernel(tc, qT, k_words, k_scales, sk, offs, out):
                 in_=q_bf[b][:].rearrange("p w j -> p (w j)"),
             )
 
-        def gather_words(b, h):
-            c0 = (b * N + h * HALF) // 16
+        def gather_scales(b):
+            c0 = b * N // PER_COLUMN
             nc.vector.tensor_copy(
-                key_words[b][h][:], pool_words[:].bitcast(U32).indirect(offsets[:, c0 : c0 + HALF // 16])
+                key_scales[b][:], pool_scales[:].bitcast(U8).indirect(offsets[:, c0 : c0 + N // PER_COLUMN])
+            )
+
+        def gather_words(b, h):
+            c0 = (b * N + h * HALF) // PER_COLUMN
+            nc.vector.tensor_copy(
+                key_words[b][h][:], pool_words[:].bitcast(U32).indirect(offsets[:, c0 : c0 + HALF // PER_COLUMN])
             )
 
         def score(b, h):
@@ -86,12 +92,6 @@ def tile_attend_wtsink_kernel(tc, qT, k_words, k_scales, sk, offs, out):
                 rhs_scale=key_scales[b][:, cols],
                 start=True,
                 stop=True,
-            )
-
-        def gather_scales(b):
-            c0 = b * N // 16
-            nc.vector.tensor_copy(
-                key_scales[b][:], pool_scales[:].bitcast(U8).indirect(offsets[:, c0 : c0 + N // 16])
             )
 
         nc.vector.tensor_copy(q_bf[0][:], q_raw[0][:].rearrange("p j w -> p w j"))
@@ -128,7 +128,7 @@ def tile_attend_wtsink_kernel(tc, qT, k_words, k_scales, sk, offs, out):
             )
         for b in range(B):
             nc.vector.reciprocal(inv[b][:], total[b][:])
-            pieces = 1 if b == 0 else 2
+            pieces = 2 if b == B - 1 else 1
             width = N // pieces
             for h in range(pieces):
                 cols = slice(h * width, (h + 1) * width)

@@ -20,6 +20,7 @@ PACK = 4
 PER_COLUMN = 16
 QUADRANT = 32
 SCALE_ROWS = D // 32
+SPREAD = P // SCALE_ROWS
 HALF = N // 2
 ROW = N + 8
 
@@ -38,7 +39,8 @@ def tile_attend_wtsink_kernel(tc, qT, k_words, k_scales, sk, offs, out):
         q_bf = [sb.tile([P, NQ, PACK], BF16, name=f"q_bf{b}", align_bytes=64) for b in range(B)]
         q_codes = [sb.tile([P, NQ], U32, name=f"q_codes{b}", align_bytes=64) for b in range(B)]
         q_scales = [sb.tile([P, NQ], U8, name=f"q_scales{b}", align_bytes=64) for b in range(B)]
-        key_scales = [sb.tile([P, N], U8, name=f"key_scales{b}", align_bytes=64) for b in range(B)]
+        picked_scales = sb.tile([P, B * N], U8, name="picked_scales", align_bytes=64)
+        key_scales = sb.tile([P, B * N // PACK], I32, name="key_scales", align_bytes=64)
         key_words = [
             [sb.tile([P, HALF], U32, name=f"key_words{b}_{h}", align_bytes=64) for h in range(2)] for b in range(B)
         ]
@@ -52,13 +54,12 @@ def tile_attend_wtsink_kernel(tc, qT, k_words, k_scales, sk, offs, out):
         scores = [psum.tile([P, N], F32, name=f"scores{b}") for b in range(B)]
 
         nc.vector.memset(pool_scales[:], 0)
+        nc.vector.memset(key_scales[:], 0)
 
         nc.sync.dma_start(q_raw[0][:], qT[0].rearrange("(p j) w -> p j w", j=PACK))
         nc.scalar.dma_start(q_raw[1][:], qT[1].rearrange("(p j) w -> p j w", j=PACK))
         nc.sync.dma_start(offsets[:], offs)
-        scale_rows = k_scales[0].bitcast(I32)
-        for r in range(4):
-            nc.sync.dma_start(pool_scales[r:P:QUADRANT, :], scale_rows[r:SCALE_ROWS:4, :])
+        nc.sync.dma_start(pool_scales[0:P:SPREAD, :], k_scales[0].bitcast(I32))
         nc.sync.dma_start(pool_words[:], k_words[0].rearrange("p n t -> p (n t)").bitcast(I32))
         with nc.allow_non_contiguous_dma(reason="one sink a query row"):
             nc.sync.dma_start(sinks[:], sk.rearrange("b q o -> q (b o)"))
@@ -68,12 +69,6 @@ def tile_attend_wtsink_kernel(tc, qT, k_words, k_scales, sk, offs, out):
                 out=q_codes[b][:].bitcast(FP8X4),
                 scales=q_scales[b][:],
                 in_=q_bf[b][:].rearrange("p w j -> p (w j)"),
-            )
-
-        def gather_scales(b):
-            c0 = b * N // PER_COLUMN
-            nc.vector.tensor_copy(
-                key_scales[b][:], pool_scales[:].bitcast(U8).indirect(offsets[:, c0 : c0 + N // PER_COLUMN])
             )
 
         def gather_words(b, h):
@@ -89,17 +84,18 @@ def tile_attend_wtsink_kernel(tc, qT, k_words, k_scales, sk, offs, out):
                 lhsT=q_codes[b][:].bitcast(FP8X4),
                 lhsT_scale=q_scales[b][:],
                 rhs=key_words[b][h][:].bitcast(FP8X4),
-                rhs_scale=key_scales[b][:, cols],
+                rhs_scale=key_scales[:].bitcast(U8)[:, b * N + h * HALF : b * N + (h + 1) * HALF],
                 start=True,
                 stop=True,
             )
 
-        nc.vector.tensor_copy(q_bf[0][:], q_raw[0][:].rearrange("p j w -> p w j"))
-        gather_scales(0)
-        quantize_queries(0)
-        nc.scalar.copy(q_bf[1][:], q_raw[1][:].rearrange("p j w -> p w j"))
-        quantize_queries(1)
-        gather_scales(1)
+        nc.vector.tensor_copy(picked_scales[:], pool_scales[:].bitcast(U8).indirect(offsets[:]))
+        for r in range(4):
+            nc.sync.dma_start(key_scales[r:P:QUADRANT, :], picked_scales[:].bitcast(I32)[SPREAD * r : P : QUADRANT, :])
+
+        for b in range(B):
+            nc.scalar.copy(q_bf[b][:], q_raw[b][:].rearrange("p j w -> p w j"))
+            quantize_queries(b)
         for b in range(B):
             nc.scalar.activation(neg[b][:, N : N + 1], sinks[:, b : b + 1], ACT.Copy, scale=-1.0)
 

@@ -20,7 +20,7 @@ PACK = 4
 PER_COLUMN = 16
 QUADRANT = 32
 SCALE_ROWS = D // 32
-SPREAD = P // SCALE_ROWS
+TABLE = P - SCALE_ROWS
 HALF = N // 2
 ROW = N + 8
 
@@ -35,15 +35,13 @@ def tile_attend_wtsink_kernel(tc, qT, k_words, k_scales, sk, offs, out):
         offsets = lists.tile([P, B * N // PER_COLUMN], U16, name="offsets")
         pool_words = sb.tile([P, T], I32, name="pool_words", align_bytes=64)
         pool_scales = sb.tile([P, T // PACK], I32, name="pool_scales", align_bytes=64)
-        q_raw = [sb.tile([P, PACK, NQ], F32, name=f"q_raw{b}") for b in range(B)]
+        q_raw = [sb.tile([P, PACK, NQ], F32, name=f"q_raw{b}", align_bytes=64) for b in range(B)]
         q_bf = [sb.tile([P, NQ, PACK], BF16, name=f"q_bf{b}", align_bytes=64) for b in range(B)]
         q_codes = [sb.tile([P, NQ], U32, name=f"q_codes{b}", align_bytes=64) for b in range(B)]
         q_scales = [sb.tile([P, NQ], U8, name=f"q_scales{b}", align_bytes=64) for b in range(B)]
         picked_scales = sb.tile([P, B * N], U8, name="picked_scales", align_bytes=64)
         key_scales = sb.tile([P, B * N // PACK], I32, name="key_scales", align_bytes=64)
-        key_words = [
-            [sb.tile([P, HALF], U32, name=f"key_words{b}_{h}", align_bytes=64) for h in range(2)] for b in range(B)
-        ]
+        key_words = {}
         sinks = sb.tile([P, B], F32, name="sinks")
         neg = [sb.tile([P, ROW], F32, name=f"neg{b}") for b in range(B)]
         neg_max = [sb.tile([P, 1], F32, name=f"neg_max{b}") for b in range(B)]
@@ -53,14 +51,14 @@ def tile_attend_wtsink_kernel(tc, qT, k_words, k_scales, sk, offs, out):
         y = [sb.tile([P, N], F32, name=f"y{b}") for b in range(B)]
         scores = [psum.tile([P, N], F32, name=f"scores{b}") for b in range(B)]
 
-        nc.vector.memset(pool_scales[:], 0)
+        nc.vector.memset(pool_scales[0:TABLE, :], 0)
         nc.vector.memset(key_scales[:], 0)
 
-        nc.sync.dma_start(q_raw[0][:], qT[0].rearrange("(p j) w -> p j w", j=PACK))
-        nc.scalar.dma_start(q_raw[1][:], qT[1].rearrange("(p j) w -> p j w", j=PACK))
+        nc.scalar.dma_start(q_raw[0][:], qT[0].rearrange("(p j) w -> p j w", j=PACK))
+        nc.sync.dma_start(pool_scales[TABLE:P, :], k_scales[0].bitcast(I32))
         nc.sync.dma_start(offsets[:], offs)
-        nc.sync.dma_start(pool_scales[0:P:SPREAD, :], k_scales[0].bitcast(I32))
         nc.sync.dma_start(pool_words[:], k_words[0].rearrange("p n t -> p (n t)").bitcast(I32))
+        nc.sync.dma_start(q_raw[1][:], qT[1].rearrange("(p j) w -> p j w", j=PACK))
         with nc.allow_non_contiguous_dma(reason="one sink a query row"):
             nc.sync.dma_start(sinks[:], sk.rearrange("b q o -> q (b o)"))
 
@@ -72,9 +70,11 @@ def tile_attend_wtsink_kernel(tc, qT, k_words, k_scales, sk, offs, out):
             )
 
         def gather_words(b, h):
+            tag = f"q_raw{b}" if (b, h) == (B - 1, 1) else f"key_words{b}_{h}"
+            key_words[b, h] = sb.tile([P, HALF], U32, name=f"key_words{b}_{h}", tag=tag, align_bytes=64)
             c0 = (b * N + h * HALF) // PER_COLUMN
             nc.vector.tensor_copy(
-                key_words[b][h][:], pool_words[:].bitcast(U32).indirect(offsets[:, c0 : c0 + HALF // PER_COLUMN])
+                key_words[b, h][:], pool_words[:].bitcast(U32).indirect(offsets[:, c0 : c0 + HALF // PER_COLUMN])
             )
 
         def score(b, h):
@@ -83,7 +83,7 @@ def tile_attend_wtsink_kernel(tc, qT, k_words, k_scales, sk, offs, out):
                 out=scores[b][:, cols],
                 lhsT=q_codes[b][:].bitcast(FP8X4),
                 lhsT_scale=q_scales[b][:],
-                rhs=key_words[b][h][:].bitcast(FP8X4),
+                rhs=key_words[b, h][:].bitcast(FP8X4),
                 rhs_scale=key_scales[:].bitcast(U8)[:, b * N + h * HALF : b * N + (h + 1) * HALF],
                 start=True,
                 stop=True,
@@ -91,7 +91,7 @@ def tile_attend_wtsink_kernel(tc, qT, k_words, k_scales, sk, offs, out):
 
         nc.vector.tensor_copy(picked_scales[:], pool_scales[:].bitcast(U8).indirect(offsets[:]))
         for r in range(4):
-            nc.sync.dma_start(key_scales[r:P:QUADRANT, :], picked_scales[:].bitcast(I32)[SPREAD * r : P : QUADRANT, :])
+            nc.sync.dma_start(key_scales[r:P:QUADRANT, :], picked_scales[:].bitcast(I32)[TABLE + r : P : 4, :])
 
         for b in range(B):
             nc.scalar.copy(q_bf[b][:], q_raw[b][:].rearrange("p j w -> p w j"))

@@ -41,7 +41,6 @@ def tile_attend_wtsink_kernel(tc, qT, k_words, k_scales, sk, offs, out):
         q_scales = [sb.tile([P, NQ], U8, name=f"q_scales{b}", align_bytes=64) for b in range(B)]
         picked_scales = sb.tile([P, B * N], U8, name="picked_scales", align_bytes=64)
         key_scales = sb.tile([P, B * N // PACK], I32, name="key_scales", align_bytes=64)
-        key_words = {}
         sinks = sb.tile([P, B], F32, name="sinks")
         neg = [sb.tile([P, ROW], F32, name=f"neg{b}") for b in range(B)]
         neg_max = [sb.tile([P, 1], F32, name=f"neg_max{b}") for b in range(B)]
@@ -69,22 +68,17 @@ def tile_attend_wtsink_kernel(tc, qT, k_words, k_scales, sk, offs, out):
                 in_=q_bf[b][:].rearrange("p w j -> p (w j)"),
             )
 
-        def gather_words(b, h):
-            tag = f"q_raw{b}" if (b, h) == (B - 1, 1) else f"key_words{b}_{h}"
-            key_words[b, h] = sb.tile([P, HALF], U32, name=f"key_words{b}_{h}", tag=tag, align_bytes=64)
-            c0 = (b * N + h * HALF) // PER_COLUMN
-            nc.vector.tensor_copy(
-                key_words[b, h][:], pool_words[:].bitcast(U32).indirect(offsets[:, c0 : c0 + HALF // PER_COLUMN])
-            )
-
-        def score(b, h):
-            cols = slice(h * HALF, (h + 1) * HALF)
+        def gather_and_score(b, first, width, tag):
+            key_words = sb.tile([P, width], U32, name=f"key_words{b}_{first}", tag=tag, align_bytes=64)
+            entry = b * N + first
+            columns = offsets[:, entry // PER_COLUMN : (entry + width) // PER_COLUMN]
+            nc.vector.tensor_copy(key_words[:], pool_words[:].bitcast(U32).indirect(columns))
             nc.tensor.matmul_mx(
-                out=scores[b][:, cols],
+                out=scores[b][:, first : first + width],
                 lhsT=q_codes[b][:].bitcast(FP8X4),
                 lhsT_scale=q_scales[b][:],
-                rhs=key_words[b, h][:].bitcast(FP8X4),
-                rhs_scale=key_scales[:].bitcast(U8)[:, b * N + h * HALF : b * N + (h + 1) * HALF],
+                rhs=key_words[:].bitcast(FP8X4),
+                rhs_scale=key_scales[:].bitcast(U8)[:, entry : entry + width],
                 start=True,
                 stop=True,
             )
@@ -99,10 +93,9 @@ def tile_attend_wtsink_kernel(tc, qT, k_words, k_scales, sk, offs, out):
         for b in range(B):
             nc.scalar.activation(neg[b][:, N : N + 1], sinks[:, b : b + 1], ACT.Copy, scale=-1.0)
 
-        for b in range(B):
-            for h in range(2):
-                gather_words(b, h)
-                score(b, h)
+        gather_and_score(0, 0, N, "key_words0")
+        gather_and_score(1, 0, HALF, "key_words1")
+        gather_and_score(1, HALF, HALF, "q_raw1")
 
         for b in range(B):
             nc.vector.tensor_scalar(

@@ -22,6 +22,7 @@ QUADRANT = 32
 SCALE_ROWS = D // 32
 TABLE = P - SCALE_ROWS
 HALF = N // 2
+SHARE = 48
 ROW = N + 8
 
 
@@ -87,9 +88,11 @@ def tile_attend_wtsink_kernel(tc, qT, k_words, k_scales, sk, offs, out):
         for r in range(4):
             nc.sync.dma_start(key_scales[r:P:QUADRANT, :], picked_scales[:].bitcast(I32)[TABLE + r : P : 4, :])
 
-        for b in range(B):
-            nc.scalar.copy(q_bf[b][:], q_raw[b][:].rearrange("p j w -> p w j"))
-            quantize_queries(b)
+        nc.scalar.copy(q_bf[0][:], q_raw[0][:].rearrange("p j w -> p w j"))
+        quantize_queries(0)
+        nc.vector.tensor_copy(q_bf[1][:, :SHARE, :], q_raw[1][:, :, :SHARE].rearrange("p j w -> p w j"))
+        nc.scalar.copy(q_bf[1][:, SHARE:, :], q_raw[1][:, :, SHARE:].rearrange("p j w -> p w j"))
+        quantize_queries(1)
         for b in range(B):
             nc.scalar.activation(neg[b][:, N : N + 1], sinks[:, b : b + 1], ACT.Copy, scale=-1.0)
 

@@ -22,7 +22,7 @@ QUADRANT = 32
 SCALE_ROWS = D // 32
 TABLE = P - SCALE_ROWS
 HALF = N // 2
-SHARE = 48
+PAIR = PACK // 2
 ROW = N + 8
 
 
@@ -36,7 +36,8 @@ def tile_attend_wtsink_kernel(tc, qT, k_words, k_scales, sk, offs, out):
         offsets = lists.tile([P, B * N // PER_COLUMN], U16, name="offsets")
         pool_words = sb.tile([P, T], I32, name="pool_words", align_bytes=64)
         pool_scales = sb.tile([P, T // PACK], I32, name="pool_scales", align_bytes=64)
-        q_raw = [sb.tile([P, PACK, NQ], F32, name=f"q_raw{b}", align_bytes=64) for b in range(B)]
+        q_first = sb.tile([P, PACK, NQ], F32, name="q_first", align_bytes=64)
+        q_last = [sb.tile([P, PAIR, NQ], F32, name=f"q_last{h}", align_bytes=64) for h in range(2)]
         q_bf = [sb.tile([P, NQ, PACK], BF16, name=f"q_bf{b}", align_bytes=64) for b in range(B)]
         q_codes = [sb.tile([P, NQ], U32, name=f"q_codes{b}", align_bytes=64) for b in range(B)]
         q_scales = [sb.tile([P, NQ], U8, name=f"q_scales{b}", align_bytes=64) for b in range(B)]
@@ -54,11 +55,13 @@ def tile_attend_wtsink_kernel(tc, qT, k_words, k_scales, sk, offs, out):
         nc.vector.memset(pool_scales[0:TABLE, :], 0)
         nc.vector.memset(key_scales[:], 0)
 
-        nc.scalar.dma_start(q_raw[0][:], qT[0].rearrange("(p j) w -> p j w", j=PACK))
+        q_rows = [qT[b].rearrange("(p j) w -> p j w", j=PACK) for b in range(B)]
+        nc.scalar.dma_start(q_first[:], q_rows[0])
+        nc.scalar.dma_start(q_last[0][:], q_rows[1][:, :PAIR, :])
         nc.sync.dma_start(pool_scales[TABLE:P, :], k_scales[0].bitcast(I32))
         nc.sync.dma_start(offsets[:], offs)
         nc.sync.dma_start(pool_words[:], k_words[0].rearrange("p n t -> p (n t)").bitcast(I32))
-        nc.sync.dma_start(q_raw[1][:], qT[1].rearrange("(p j) w -> p j w", j=PACK))
+        nc.sync.dma_start(q_last[1][:], q_rows[1][:, PAIR:, :])
         with nc.allow_non_contiguous_dma(reason="one sink a query row"):
             nc.sync.dma_start(sinks[:], sk.rearrange("b q o -> q (b o)"))
 
@@ -88,17 +91,17 @@ def tile_attend_wtsink_kernel(tc, qT, k_words, k_scales, sk, offs, out):
         for r in range(4):
             nc.sync.dma_start(key_scales[r:P:QUADRANT, :], picked_scales[:].bitcast(I32)[TABLE + r : P : 4, :])
 
-        nc.scalar.copy(q_bf[0][:], q_raw[0][:].rearrange("p j w -> p w j"))
+        nc.scalar.copy(q_bf[0][:], q_first[:].rearrange("p j w -> p w j"))
         quantize_queries(0)
-        nc.vector.tensor_copy(q_bf[1][:, :SHARE, :], q_raw[1][:, :, :SHARE].rearrange("p j w -> p w j"))
-        nc.scalar.copy(q_bf[1][:, SHARE:, :], q_raw[1][:, :, SHARE:].rearrange("p j w -> p w j"))
+        for h in range(2):
+            nc.scalar.copy(q_bf[1][:, :, h * PAIR : (h + 1) * PAIR], q_last[h][:].rearrange("p j w -> p w j"))
         quantize_queries(1)
         for b in range(B):
             nc.scalar.activation(neg[b][:, N : N + 1], sinks[:, b : b + 1], ACT.Copy, scale=-1.0)
 
         gather_and_score(0, 0, N, "key_words0")
         gather_and_score(1, 0, HALF, "key_words1")
-        gather_and_score(1, HALF, HALF, "q_raw1")
+        gather_and_score(1, HALF, HALF, "q_last1")
 
         for b in range(B):
             nc.vector.tensor_scalar(

from contextlib import ExitStack

import concourse.mybir as mybir

B, N, T, D, NQ = 2, 512, 2048, 512, 128
FLOPS = 2 * B * NQ * N * D

F32 = mybir.dt.float32
BF16 = mybir.dt.bfloat16
I32 = mybir.dt.int32
U32 = mybir.dt.uint32
U16 = mybir.dt.uint16
U8 = mybir.dt.uint8
FP8X4 = mybir.dt.float8_e4m3fn_x4
ALU = mybir.AluOpType
ACT = mybir.ActivationFunctionType

P = 128
PACK = 4
PER_COLUMN = 16
QUADRANT = 32
SCALE_ROWS = D // 32
TABLE = P - SCALE_ROWS
HALF = N // 2
PAIR = PACK // 2
ROW = N + 8


def tile_attend_wtsink_kernel(tc, qT, k_words, k_scales, sk, offs, out):
    nc = tc.nc
    with ExitStack() as ctx:
        lists = ctx.enter_context(tc.tile_pool(name="lists", bufs=1))
        sb = ctx.enter_context(tc.tile_pool(name="sb", bufs=1))
        psum = ctx.enter_context(tc.psum_pool(name="psum", bufs=1))

        offsets = lists.tile([P, B * N // PER_COLUMN], U16, name="offsets")
        pool_words = sb.tile([P, T], I32, name="pool_words", align_bytes=64)
        pool_scales = sb.tile([P, T // PACK], I32, name="pool_scales", align_bytes=64)
        q_first = sb.tile([P, PACK, NQ], F32, name="q_first", align_bytes=64)
        q_last = [sb.tile([P, PAIR, NQ], F32, name=f"q_last{h}", align_bytes=64) for h in range(2)]
        q_bf = [sb.tile([P, NQ, PACK], BF16, name=f"q_bf{b}", align_bytes=64) for b in range(B)]
        q_codes = [sb.tile([P, NQ], U32, name=f"q_codes{b}", align_bytes=64) for b in range(B)]
        q_scales = [sb.tile([P, NQ], U8, name=f"q_scales{b}", align_bytes=64) for b in range(B)]
        picked_scales = sb.tile([P, B * N], U8, name="picked_scales", align_bytes=64)
        key_scales = sb.tile([P, B * N // PACK], I32, name="key_scales", align_bytes=64)
        sinks = sb.tile([P, B], F32, name="sinks")
        neg = [sb.tile([P, ROW], F32, name=f"neg{b}") for b in range(B)]
        neg_max = [sb.tile([P, 1], F32, name=f"neg_max{b}") for b in range(B)]
        e = [sb.tile([P, ROW], F32, name=f"e{b}") for b in range(B)]
        total = [sb.tile([P, 1], F32, name=f"total{b}") for b in range(B)]
        inv = [sb.tile([P, 1], F32, name=f"inv{b}") for b in range(B)]
        y = [sb.tile([P, N], F32, name=f"y{b}") for b in range(B)]
        scores = [psum.tile([P, N], F32, name=f"scores{b}") for b in range(B)]

        nc.vector.memset(pool_scales[0:TABLE, :], 0)
        nc.vector.memset(key_scales[:], 0)

        q_rows = [qT[b].rearrange("(p j) w -> p j w", j=PACK) for b in range(B)]
        nc.scalar.dma_start(q_first[:], q_rows[0])
        nc.scalar.dma_start(q_last[0][:], q_rows[1][:, :PAIR, :])
        nc.sync.dma_start(pool_scales[TABLE:P, :], k_scales[0].bitcast(I32))
        nc.sync.dma_start(offsets[:], offs)
        nc.sync.dma_start(pool_words[:], k_words[0].rearrange("p n t -> p (n t)").bitcast(I32))
        nc.sync.dma_start(q_last[1][:], q_rows[1][:, PAIR:, :])
        with nc.allow_non_contiguous_dma(reason="one sink a query row"):
            nc.sync.dma_start(sinks[:], sk.rearrange("b q o -> q (b o)"))

        def quantize_queries(b):
            nc.vector.quantize_mx(
                out=q_codes[b][:].bitcast(FP8X4),
                scales=q_scales[b][:],
                in_=q_bf[b][:].rearrange("p w j -> p (w j)"),
            )

        def gather_and_score(b, first, width, tag):
            key_words = sb.tile([P, width], U32, name=f"key_words{b}_{first}", tag=tag, align_bytes=64)
            entry = b * N + first
            columns = offsets[:, entry // PER_COLUMN : (entry + width) // PER_COLUMN]
            nc.vector.tensor_copy(key_words[:], pool_words[:].bitcast(U32).indirect(columns))
            nc.tensor.matmul_mx(
                out=scores[b][:, first : first + width],
                lhsT=q_codes[b][:].bitcast(FP8X4),
                lhsT_scale=q_scales[b][:],
                rhs=key_words[:].bitcast(FP8X4),
                rhs_scale=key_scales[:].bitcast(U8)[:, entry : entry + width],
                start=True,
                stop=True,
            )

        nc.vector.tensor_copy(picked_scales[:], pool_scales[:].bitcast(U8).indirect(offsets[:]))
        for r in range(4):
            nc.sync.dma_start(key_scales[r:P:QUADRANT, :], picked_scales[:].bitcast(I32)[TABLE + r : P : 4, :])

        nc.scalar.copy(q_bf[0][:], q_first[:].rearrange("p j w -> p w j"))
        quantize_queries(0)
        for h in range(2):
            nc.scalar.copy(q_bf[1][:, :, h * PAIR : (h + 1) * PAIR], q_last[h][:].rearrange("p j w -> p w j"))
        quantize_queries(1)
        for b in range(B):
            nc.scalar.activation(neg[b][:, N : N + 1], sinks[:, b : b + 1], ACT.Copy, scale=-1.0)

        gather_and_score(0, 0, N, "key_words0")
        gather_and_score(1, 0, HALF, "key_words1")
        gather_and_score(1, HALF, HALF, "q_last1")

        for b in range(B):
            nc.vector.tensor_scalar(
                out=neg[b][:, 0:N],
                in0=scores[b][:],
                scalar1=-1.0,
                scalar2=neg[b][:, N : N + 1],
                op0=ALU.mult,
                op1=ALU.min,
                accum_out=neg_max[b][:],
            )
            nc.scalar.activation(
                e[b][:, 0 : N + 1],
                neg[b][:, 0 : N + 1],
                ACT.Exp,
                bias=neg_max[b][:],
                scale=-1.0,
                accum_out=total[b][:],
            )
        for b in range(B):
            nc.vector.reciprocal(inv[b][:], total[b][:])
            pieces = 2 if b == B - 1 else 1
            width = N // pieces
            for h in range(pieces):
                cols = slice(h * width, (h + 1) * width)
                nc.vector.tensor_scalar(
                    out=y[b][:, cols], in0=e[b][:, cols], scalar1=inv[b][:], scalar2=None, op0=ALU.mult
                )
                queue = nc.scalar if h == 1 else nc.sync
                queue.dma_start(out[b][:, cols], y[b][:, cols])
